import numpy as np
import ml_dtypes


def mxq(x, axis, fmt="e4m3"):
    dtype, down = {"e4m3": (ml_dtypes.float8_e4m3fn, 7), "e5m2": (ml_dtypes.float8_e5m2, 14)}[fmt]
    v = np.moveaxis(np.asarray(x, np.float32).astype(ml_dtypes.bfloat16).astype(np.float64), axis, -1)
    blocks = v.reshape(v.shape[:-1] + (-1, 32))
    amax = np.abs(blocks).max(-1, keepdims=True)
    byte = np.maximum(np.where(amax > 0, np.frexp(amax)[1] - 1 + 127, 0) - down, 1)
    scale = np.exp2(byte - 127.0)
    codes = (blocks / scale).astype(np.float32).astype(dtype).astype(np.float64)
    return np.moveaxis((codes * scale).reshape(v.shape), -1, axis)


WIDE = False


def mx_kscale(k):
    if not WIDE:
        return np.ones(k)
    levels = np.array([10, -10, 5, -5, 0])
    if k % 512:
        return np.exp2(np.random.permutation(np.resize(levels, k // 32))).repeat(32)
    a = np.empty((k // 512, 16))
    for p in range(k // 512):
        a[p, :8] = np.random.permutation(np.resize(levels, 8))
        for g in range(8):
            far = levels[np.abs(levels - a[p, g]) >= 10]
            a[p, g + 8] = far[np.random.randint(len(far))]
    return np.exp2(a.ravel()).repeat(32)


def f64(x):
    return np.asarray(x).astype(np.float64)


def striped(idx):
    return np.tile(np.asarray(idx).reshape(-1, 16).T, (8, 1)).astype(np.uint16)


def unstriped(offs):
    return offs[:16].T.reshape(-1).astype(np.int64)


E2M1 = np.array([0.0, 0.5, 1.0, 1.5, 2.0, 3.0, 4.0, 6.0, -0.0, -0.5, -1.0, -1.5, -2.0, -3.0, -4.0, -6.0])


def pack_weight(w, fmt):
    k, n = w.shape
    w = f64(np.asarray(w, np.float32).astype(ml_dtypes.bfloat16)).reshape(k // 32, 32, n)
    amax = np.abs(w).max(1)
    if fmt == "e4m3":
        byte = np.frexp(amax)[1] - 1 + 127 - 7
    else:
        mant, ex = np.frexp(amax / 6.0)
        byte = np.where(mant > 0.5, ex, ex - 1) + 127
    byte = np.clip(np.where(amax > 0, byte, 1), 1, 254)
    scaled = (w * np.exp2(127.0 - byte)[:, None, :]).reshape(k, n).astype(np.float32)
    by_word = np.ascontiguousarray(scaled.reshape(k // 512, 128, 4, n).transpose(0, 1, 3, 2))
    if fmt == "e4m3":
        words = by_word.astype(ml_dtypes.float8_e4m3fn).view(np.uint8)
    else:
        c = by_word.astype(ml_dtypes.float4_e2m1fn).view(np.uint8) & 0xF
        words = (c[..., 0::2] | (c[..., 1::2] << 4)).reshape(k // 512, 128, 2 * n)
    return np.ascontiguousarray(words), np.ascontiguousarray(byte.astype(np.uint8).reshape(k // 512, 16, n))


def unpack_weight(words, scales, fmt):
    g, _, n = scales.shape
    words = np.ascontiguousarray(words).reshape(g, 128, n, -1)
    if fmt == "e4m3":
        vals = words.view(ml_dtypes.float8_e4m3fn).astype(np.float64)
    else:
        nib = np.empty((g, 128, n, 4), np.uint8)
        nib[..., 0::2] = words & 0xF
        nib[..., 1::2] = words >> 4
        vals = E2M1[nib]
    vals = vals * np.repeat(np.exp2(scales.astype(np.float64) - 127.0), 8, axis=1)[..., None]
    return vals.transpose(0, 1, 3, 2).reshape(g * 512, n)


def softplus(v):
    return np.log(1.0 + np.exp(v))


def sigmoid(v):
    return 1.0 / (1.0 + np.exp(-v))


D, E, T, I, Q = 512, 512, 2048, 512, 128


def setup_inputs():
    n = np.random.standard_normal
    idx = np.random.permutation(T)[:I]
    fd = mx_kscale(D)
    fe = mx_kscale(E)
    keysp = pack_weight(n((D, T)) / fd[:, None], "e4m3")
    valsp = pack_weight(n((E, T)) / fe[:, None], "e4m3")
    return {
        "query": (n((D, Q)) * 0.6 / np.sqrt(D) * fd[:, None]).astype(np.float32),
        "query2": (n((D, Q)) * 1.0 / np.sqrt(D) * fd[:, None]).astype(np.float32),
        "keys_words": keysp[0],
        "keys_scales": keysp[1],
        "strict": (np.random.uniform(0.4, 1.2, (Q, 1))).astype(np.float32),
        "gout": (n((E, Q)) * 1 / np.sqrt(E) * fe[:, None]).astype(np.float32),
        "vals_words": valsp[0],
        "vals_scales": valsp[1],
        "dquery2": (n((D, Q)) * 1.0 / np.sqrt(D) * fd[:, None]).astype(np.float32),
        "base": (0.5 * n((Q, T))).astype(np.float32),
        "offs": striped(idx),
    }


def reference(query, query2, keys_words, keys_scales, strict, gout, vals_words, vals_scales, dquery2, base, offs):
    idx = unstriped(offs)
    keysu = unpack_weight(keys_words, keys_scales, "e4m3")
    valsu = unpack_weight(vals_words, vals_scales, "e4m3")
    queryq = mxq(f64(query), 0, "e4m3")
    keysidxg = keysu[:, idx]
    a = queryq.T @ keysidxg
    query2q = mxq(f64(query2), 0, "e4m3")
    b = query2q.T @ keysidxg
    dquery2q = mxq(f64(dquery2), 0, "e4m3")
    tb = dquery2q.T @ keysidxg
    s = a - softplus(b) * f64(strict)
    p = np.exp(s - np.max(s, axis=1, keepdims=True))
    z = np.sum(p, axis=1, keepdims=True)
    goutq = mxq(f64(gout), 0, "e4m3")
    valsidxg = valsu[:, idx]
    c0 = goutq.T @ valsidxg
    dz = np.sum(c0 * p / np.square(z) * (-1.0), axis=1, keepdims=True)
    dp = c0 / z + dz
    ds = dp * p
    ts = tb * sigmoid(b) * f64(strict) * (-1.0)
    tp = ts * p
    tz = np.sum(tp, axis=1, keepdims=True)
    tdz = np.sum((tp * c0 - tz * z * 2.0 * c0 * p / np.square(z)) / np.square(z) * (-1.0), axis=1, keepdims=True)
    tdp = tz * c0 / np.square(z) * (-1.0) + tdz
    tds = tdp * p + tp * dp
    tdb = tds * (-1.0) * f64(strict) * sigmoid(b) + tb * sigmoid(b) * (1.0 - sigmoid(b)) * ds * (-1.0) * f64(strict)
    gs = tdb * 512.0
    gf = np.zeros((Q, T))
    gf[:, idx] = gs
    y = f64(base) + gf
    return y

@@ -1,0 +1,169 @@
+from contextlib import ExitStack
+
+import concourse.mybir as mybir
+
+D, T, I, Q = 512, 2048, 512, 128
+FLOPS = 4 * 2 * D * Q * I
+
+F32 = mybir.dt.float32
+BF16 = mybir.dt.bfloat16
+I32 = mybir.dt.int32
+U32 = mybir.dt.uint32
+U16 = mybir.dt.uint16
+U8 = mybir.dt.uint8
+FP8X4 = mybir.dt.float8_e4m3fn_x4
+ALU = mybir.AluOpType
+ACT = mybir.ActivationFunctionType
+AX = mybir.AxisListType
+
+P = 128
+PACK = 4
+LN_FLOOR = 2.0 ** -40
+OUT_CHUNKS = (512, 512, 512, 512)
+
+
+def tile_attend_hvheldback_s_kernel(tc, query, query2, keys_words, keys_scales, strict, gout,
+                                     vals_words, vals_scales, dquery2, base, offs, out):
+    nc = tc.nc
+    with ExitStack() as ctx:
+        keep = ctx.enter_context(tc.tile_pool(name="keep", bufs=1))
+        psum = ctx.enter_context(tc.psum_pool(name="psum", bufs=1))
+
+        def sb(name, cols, dtype):
+            return keep.tile([P, cols], dtype, name=name, align_bytes=64)
+
+        offsets = keep.tile([P, I // 16], U16, name="offsets")
+        nc.sync.dma_start(offsets[:], offs)
+
+        def load_rows(name, src):
+            raw = keep.tile([P, PACK, Q], F32, name=name + "_raw")
+            nc.sync.dma_start(out=raw[:], in_=src.rearrange("(p j) q -> p j q", j=PACK))
+            return raw
+
+        def load_words(name, src):
+            words = sb(name + "_words", T, I32)
+            nc.sync.dma_start(out=words[:], in_=src[0].rearrange("p n t -> p (n t)").bitcast(I32))
+            return words
+
+        def load_scales(name, src, clear, queue):
+            plane = sb(name + "_scales", T, U8)
+            clear.memset(plane[:].bitcast(I32), 0)
+            for quad in range(4):
+                queue.dma_start(out=plane[32 * quad:32 * quad + 4, :].bitcast(I32),
+                                in_=src[0, 4 * quad:4 * quad + 4, :].bitcast(I32))
+            return plane
+
+        def quantise(name, raw):
+            grouped = keep.tile([P, Q, PACK], BF16, name=name + "_bf", align_bytes=64)
+            nc.scalar.copy(out=grouped[:], in_=raw[:].rearrange("p j q -> p q j"))
+            codes = sb(name + "_codes", Q, U32)
+            scales = sb(name + "_qs", Q, U8)
+            nc.vector.quantize_mx(out=codes[:].bitcast(FP8X4), scales=scales[:],
+                                  in_=grouped[:].rearrange("p q j -> p (q j)"))
+            return codes, scales
+
+        def gather(name, window, dtype):
+            picked = sb(name, I, dtype)
+            nc.vector.tensor_copy(picked[:], window.indirect(offsets[:]))
+            return picked
+
+        def product(name, rows, words, scales):
+            bank = psum.tile([P, I], F32, name=name)
+            nc.tensor.matmul_mx(out=bank[:], lhsT=rows[0][:].bitcast(FP8X4), lhsT_scale=rows[1][:],
+                                rhs=words[:].bitcast(FP8X4), rhs_scale=scales[:], start=True, stop=True)
+            return bank
+
+        key_plane = load_scales("keys", keys_scales, nc.gpsimd, nc.scalar)
+        q2_raw = load_rows("q2", query2)
+        key_words = load_words("keys", keys_words)
+        q_raw = load_rows("q", query)
+        val_plane = load_scales("vals", vals_scales, nc.vector, nc.sync)
+        dq2_raw = load_rows("dq2", dquery2)
+        go_raw = load_rows("go", gout)
+        k = keep.tile([P, 1], F32, name="k")
+        nc.sync.dma_start(out=k[:], in_=strict)
+        val_words = load_words("vals", vals_words)
+        base_sb = sb("base_sb", T, F32)
+        nc.sync.dma_start(out=base_sb[:], in_=base)
+
+        placed = sb("placed", T, F32)
+        nc.vector.memset(placed[:], 0.0)
+
+        key_s = gather("key_s", key_plane[:], U8)
+        q2 = quantise("q2", q2_raw)
+        key_w = gather("key_w", key_words[:].bitcast(U32), U32)
+        b = product("b", q2, key_w, key_s)
+        sn = sb("sn", I, F32)
+        nc.scalar.activation(out=sn[:], in_=b[:], func=ACT.Sigmoid, scale=-1.0)
+
+        q1 = quantise("q", q_raw)
+        dq2 = quantise("dq2", dq2_raw)
+        go = quantise("go", go_raw)
+        a = product("a", q1, key_w, key_s)
+        tb = product("tb", dq2, key_w, key_s)
+
+        floor = keep.tile([P, 1], F32, name="floor")
+        nc.vector.memset(floor[:], LN_FLOOR)
+        lsn = sb("lsn", I, F32)
+        nc.scalar.activation(out=lsn[:], in_=sn[:], func=ACT.Ln, bias=floor[:])
+
+        val_s = gather("val_s", val_plane[:], U8)
+        val_w = gather("val_w", val_words[:].bitcast(U32), U32)
+        c0 = product("c0", go, val_w, val_s)
+
+        nk1 = keep.tile([P, 1], F32, name="nk1")
+        nc.vector.tensor_scalar(nk1[:], k[:], -1.0, -1.0, ALU.mult, ALU.add)
+        nk512 = keep.tile([P, 1], F32, name="nk512")
+        nc.vector.tensor_scalar(nk512[:], k[:], -512.0, None, ALU.mult)
+
+        ts = sb("ts", I, F32)
+        nc.vector.scalar_tensor_tensor(ts[:], sn[:], -1.0, tb[:], ALU.add, ALU.mult)
+
+        nsp = sb("nsp", I, F32)
+        nc.vector.scalar_tensor_tensor(nsp[:], b[:], -1.0, lsn[:], ALU.mult, ALU.min)
+        s = sb("s", I, F32)
+        nc.vector.scalar_tensor_tensor(s[:], nsp[:], k[:], a[:], ALU.mult, ALU.add)
+        nmax = keep.tile([P, 1], F32, name="nmax")
+        nc.vector.tensor_reduce(nmax[:], s[:], AX.X, ALU.max, negate=True)
+        p = sb("p", I, F32)
+        z = keep.tile([P, 1], F32, name="z")
+        nc.scalar.activation(out=p[:], in_=s[:], func=ACT.Exp, bias=nmax[:], accum_out=z[:])
+
+        h = sb("h", I, F32)
+        nc.vector.scalar_tensor_tensor(h[:], ts[:], nk1[:], tb[:], ALU.mult, ALU.subtract)
+
+        pc = sb("pc", I, F32)
+        ncz = keep.tile([P, 1], F32, name="ncz")
+        nc.vector.scalar_tensor_tensor(pc[:], p[:], -1.0, c0[:], ALU.mult, ALU.mult, accum_out=ncz[:])
+        nsig = sb("nsig", I, F32)
+        nc.scalar.activation(out=nsig[:], in_=sn[:], func=ACT.Copy, bias=-1.0)
+        rz = keep.tile([P, 1], F32, name="rz")
+        nc.vector.reciprocal(rz[:], z[:])
+        tp = sb("tp", I, F32)
+        tz = keep.tile([P, 1], F32, name="tz")
+        nc.vector.scalar_tensor_tensor(tp[:], p[:], k[:], ts[:], ALU.mult, ALU.mult, accum_out=tz[:])
+        cc = sb("cc", I, F32)
+        nc.scalar.activation(out=cc[:], in_=c0[:], func=ACT.Identity, scale=z[:], bias=ncz[:])
+        tmean = keep.tile([P, 1], F32, name="tmean")
+        nc.scalar.activation(out=tmean[:], in_=tz[:], func=ACT.Copy, scale=rz[:])
+        tc0 = sb("tc0", I, F32)
+        v = keep.tile([P, 1], F32, name="v")
+        nc.vector.scalar_tensor_tensor(tc0[:], tp[:], rz[:], cc[:], ALU.mult, ALU.mult, accum_out=v[:])
+        y = sb("y", I, F32)
+        nc.vector.scalar_tensor_tensor(y[:], h[:], tmean[:], cc[:], ALU.add, ALU.mult)
+        x = sb("x", I, F32)
+        nc.vector.scalar_tensor_tensor(x[:], y[:], v[:], nsig[:], ALU.add, ALU.mult)
+        nc.vector.tensor_tensor(placed[:].indirect(offsets[:]), p[:], x[:], ALU.mult)
+
+        f1 = keep.tile([P, 1], F32, name="f1")
+        nc.scalar.activation(out=f1[:], in_=rz[:], func=ACT.Copy, scale=nk512[:])
+        f2 = keep.tile([P, 1], F32, name="f2")
+        nc.scalar.activation(out=f2[:], in_=f1[:], func=ACT.Copy, scale=rz[:])
+
+        start = 0
+        for n, width in enumerate(OUT_CHUNKS):
+            cols = slice(start, start + width)
+            res = sb("res%d" % n, width, F32)
+            nc.vector.scalar_tensor_tensor(res[:], placed[:, cols], f2[:], base_sb[:, cols], ALU.mult, ALU.add)
+            nc.sync.dma_start(out=out[:, cols], in_=res[:])
+            start = start + width

@@ -19,7 +19,7 @@ AX = mybir.AxisListType
 P = 128
 PACK = 4
 LN_FLOOR = 2.0 ** -40
-OUT_CHUNKS = (512, 512, 512, 512)
+OUT_CHUNKS = (640, 640, 512, 256)
 
 
 def tile_attend_hvheldback_s_kernel(tc, query, query2, keys_words, keys_scales, strict, gout,
@@ -29,8 +29,8 @@ def tile_attend_hvheldback_s_kernel(tc, query, query2, keys_words, keys_scales, 
         keep = ctx.enter_context(tc.tile_pool(name="keep", bufs=1))
         psum = ctx.enter_context(tc.psum_pool(name="psum", bufs=1))
 
-        def sb(name, cols, dtype):
-            return keep.tile([P, cols], dtype, name=name, align_bytes=64)
+        def sb(name, cols, dtype, tag=""):
+            return keep.tile([P, cols], dtype, name=name, tag=tag or name, align_bytes=64)
 
         offsets = keep.tile([P, I // 16], U16, name="offsets")
         nc.sync.dma_start(offsets[:], offs)
@@ -45,25 +45,28 @@ def tile_attend_hvheldback_s_kernel(tc, query, query2, keys_words, keys_scales, 
             nc.sync.dma_start(out=words[:], in_=src[0].rearrange("p n t -> p (n t)").bitcast(I32))
             return words
 
-        def load_scales(name, src, clear, queue):
+        def load_scales(name, src, clear, queues):
             plane = sb(name + "_scales", T, U8)
             clear.memset(plane[:].bitcast(I32), 0)
             for quad in range(4):
-                queue.dma_start(out=plane[32 * quad:32 * quad + 4, :].bitcast(I32),
+                queues[quad].dma_start(out=plane[32 * quad:32 * quad + 4, :].bitcast(I32),
                                 in_=src[0, 4 * quad:4 * quad + 4, :].bitcast(I32))
             return plane
 
-        def quantise(name, raw):
+        def interleave(name, raw, copy):
             grouped = keep.tile([P, Q, PACK], BF16, name=name + "_bf", align_bytes=64)
-            nc.scalar.copy(out=grouped[:], in_=raw[:].rearrange("p j q -> p q j"))
+            copy(out=grouped[:], in_=raw[:].rearrange("p j q -> p q j"))
+            return grouped
+
+        def quantise(name, grouped):
             codes = sb(name + "_codes", Q, U32)
             scales = sb(name + "_qs", Q, U8)
             nc.vector.quantize_mx(out=codes[:].bitcast(FP8X4), scales=scales[:],
                                   in_=grouped[:].rearrange("p q j -> p (q j)"))
             return codes, scales
 
-        def gather(name, window, dtype):
-            picked = sb(name, I, dtype)
+        def gather(name, window, dtype, tag=""):
+            picked = sb(name, I, dtype, tag)
             nc.vector.tensor_copy(picked[:], window.indirect(offsets[:]))
             return picked
 
@@ -73,92 +76,100 @@ def tile_attend_hvheldback_s_kernel(tc, query, query2, keys_words, keys_scales, 
                                 rhs=words[:].bitcast(FP8X4), rhs_scale=scales[:], start=True, stop=True)
             return bank
 
-        key_plane = load_scales("keys", keys_scales, nc.gpsimd, nc.scalar)
+        halves = (slice(0, I // 2), slice(I // 2, I))
+
+        def col(name):
+            return keep.tile([P, 1], F32, name=name)
+
         q2_raw = load_rows("q2", query2)
+        k = col("k")
+        nc.sync.dma_start(out=k[:], in_=strict)
+        key_plane = load_scales("keys", keys_scales, nc.gpsimd, (nc.scalar, nc.scalar, nc.sync, nc.sync))
         key_words = load_words("keys", keys_words)
         q_raw = load_rows("q", query)
-        val_plane = load_scales("vals", vals_scales, nc.vector, nc.sync)
         dq2_raw = load_rows("dq2", dquery2)
         go_raw = load_rows("go", gout)
-        k = keep.tile([P, 1], F32, name="k")
-        nc.sync.dma_start(out=k[:], in_=strict)
+        val_plane = load_scales("vals", vals_scales, nc.vector, (nc.sync,) * 4)
         val_words = load_words("vals", vals_words)
         base_sb = sb("base_sb", T, F32)
         nc.sync.dma_start(out=base_sb[:], in_=base)
 
+        floor = col("floor")
+        nc.vector.memset(floor[:], LN_FLOOR)
+        warm = col("warm")
+        nc.scalar.activation(out=warm[:], in_=floor[:], func=ACT.Sigmoid)
         placed = sb("placed", T, F32)
         nc.vector.memset(placed[:], 0.0)
 
+        q2 = quantise("q2", interleave("q2", q2_raw, nc.vector.tensor_copy))
+        q_bf = interleave("q", q_raw, nc.scalar.copy)
+        dq2_bf = interleave("dq2", dq2_raw, nc.scalar.copy)
         key_s = gather("key_s", key_plane[:], U8)
-        q2 = quantise("q2", q2_raw)
+        nk1 = col("nk1")
+        nc.vector.tensor_scalar(nk1[:], k[:], -1.0, -1.0, ALU.mult, ALU.add)
         key_w = gather("key_w", key_words[:].bitcast(U32), U32)
         b = product("b", q2, key_w, key_s)
         sn = sb("sn", I, F32)
         nc.scalar.activation(out=sn[:], in_=b[:], func=ACT.Sigmoid, scale=-1.0)
-
-        q1 = quantise("q", q_raw)
-        dq2 = quantise("dq2", dq2_raw)
-        go = quantise("go", go_raw)
-        a = product("a", q1, key_w, key_s)
-        tb = product("tb", dq2, key_w, key_s)
-
-        floor = keep.tile([P, 1], F32, name="floor")
-        nc.vector.memset(floor[:], LN_FLOOR)
         lsn = sb("lsn", I, F32)
         nc.scalar.activation(out=lsn[:], in_=sn[:], func=ACT.Ln, bias=floor[:])
 
+        a = product("a", quantise("q", q_bf), key_w, key_s)
+        go_bf = interleave("go", go_raw, nc.vector.tensor_copy)
+        tb = product("tb", quantise("dq2", dq2_bf), key_w, key_s)
         val_s = gather("val_s", val_plane[:], U8)
-        val_w = gather("val_w", val_words[:].bitcast(U32), U32)
-        c0 = product("c0", go, val_w, val_s)
-
-        nk1 = keep.tile([P, 1], F32, name="nk1")
-        nc.vector.tensor_scalar(nk1[:], k[:], -1.0, -1.0, ALU.mult, ALU.add)
-        nk512 = keep.tile([P, 1], F32, name="nk512")
-        nc.vector.tensor_scalar(nk512[:], k[:], -512.0, None, ALU.mult)
-
-        ts = sb("ts", I, F32)
-        nc.vector.scalar_tensor_tensor(ts[:], sn[:], -1.0, tb[:], ALU.add, ALU.mult)
+        go = quantise("go", go_bf)
 
         nsp = sb("nsp", I, F32)
         nc.vector.scalar_tensor_tensor(nsp[:], b[:], -1.0, lsn[:], ALU.mult, ALU.min)
         s = sb("s", I, F32)
         nc.vector.scalar_tensor_tensor(s[:], nsp[:], k[:], a[:], ALU.mult, ALU.add)
-        nmax = keep.tile([P, 1], F32, name="nmax")
+        nmax = col("nmax")
         nc.vector.tensor_reduce(nmax[:], s[:], AX.X, ALU.max, negate=True)
         p = sb("p", I, F32)
-        z = keep.tile([P, 1], F32, name="z")
+        z = col("z")
         nc.scalar.activation(out=p[:], in_=s[:], func=ACT.Exp, bias=nmax[:], accum_out=z[:])
 
+        ts = sb("ts", I, F32)
+        nc.vector.scalar_tensor_tensor(ts[:], sn[:], -1.0, tb[:], ALU.add, ALU.mult)
         h = sb("h", I, F32)
         nc.vector.scalar_tensor_tensor(h[:], ts[:], nk1[:], tb[:], ALU.mult, ALU.subtract)
 
-        pc = sb("pc", I, F32)
-        ncz = keep.tile([P, 1], F32, name="ncz")
-        nc.vector.scalar_tensor_tensor(pc[:], p[:], -1.0, c0[:], ALU.mult, ALU.mult, accum_out=ncz[:])
-        nsig = sb("nsig", I, F32)
-        nc.scalar.activation(out=nsig[:], in_=sn[:], func=ACT.Copy, bias=-1.0)
-        rz = keep.tile([P, 1], F32, name="rz")
-        nc.vector.reciprocal(rz[:], z[:])
+        val_w = gather("val_w", val_words[:].bitcast(U32), U32, "nsp")
+        c0 = product("c0", go, val_w, val_s)
+
         tp = sb("tp", I, F32)
-        tz = keep.tile([P, 1], F32, name="tz")
+        tz = col("tz")
         nc.vector.scalar_tensor_tensor(tp[:], p[:], k[:], ts[:], ALU.mult, ALU.mult, accum_out=tz[:])
+        rz = col("rz")
+        nc.vector.reciprocal(rz[:], z[:])
+        pc = sb("pc", I, F32)
+        ncz = col("ncz")
+        nc.vector.scalar_tensor_tensor(pc[:], p[:], -1.0, c0[:], ALU.mult, ALU.mult, accum_out=ncz[:])
         cc = sb("cc", I, F32)
-        nc.scalar.activation(out=cc[:], in_=c0[:], func=ACT.Identity, scale=z[:], bias=ncz[:])
-        tmean = keep.tile([P, 1], F32, name="tmean")
-        nc.scalar.activation(out=tmean[:], in_=tz[:], func=ACT.Copy, scale=rz[:])
+        for half in halves:
+            nc.scalar.activation(out=cc[:, half], in_=c0[:, half], func=ACT.Identity, scale=z[:], bias=ncz[:])
         tc0 = sb("tc0", I, F32)
-        v = keep.tile([P, 1], F32, name="v")
-        nc.vector.scalar_tensor_tensor(tc0[:], tp[:], rz[:], cc[:], ALU.mult, ALU.mult, accum_out=v[:])
+        uz = col("uz")
+        nc.vector.scalar_tensor_tensor(tc0[:], tp[:], 1.0, c0[:], ALU.mult, ALU.mult, accum_out=uz[:])
+        tmean = col("tmean")
+        nc.scalar.activation(out=tmean[:], in_=tz[:], func=ACT.Copy, scale=rz[:])
+        v = col("v")
+        nc.scalar.activation(out=v[:], in_=ncz[:], func=ACT.Identity, scale=tmean[:], bias=uz[:])
+        sig = sb("sig", I, F32, "s")
+        nc.scalar.activation(out=sig[:], in_=sn[:], func=ACT.Copy, scale=-512.0, bias=512.0)
         y = sb("y", I, F32)
-        nc.vector.scalar_tensor_tensor(y[:], h[:], tmean[:], cc[:], ALU.add, ALU.mult)
+        for half in halves:
+            nc.vector.scalar_tensor_tensor(y[:, half], h[:, half], tmean[:], cc[:, half], ALU.add, ALU.mult)
         x = sb("x", I, F32)
-        nc.vector.scalar_tensor_tensor(x[:], y[:], v[:], nsig[:], ALU.add, ALU.mult)
+        for half in halves:
+            nc.vector.scalar_tensor_tensor(x[:, half], y[:, half], v[:], sig[:, half], ALU.add, ALU.mult)
         nc.vector.tensor_tensor(placed[:].indirect(offsets[:]), p[:], x[:], ALU.mult)
 
-        f1 = keep.tile([P, 1], F32, name="f1")
-        nc.scalar.activation(out=f1[:], in_=rz[:], func=ACT.Copy, scale=nk512[:])
-        f2 = keep.tile([P, 1], F32, name="f2")
-        nc.scalar.activation(out=f2[:], in_=f1[:], func=ACT.Copy, scale=rz[:])
+        f1 = col("f1")
+        nc.scalar.activation(out=f1[:], in_=rz[:], func=ACT.Square)
+        f2 = col("f2")
+        nc.scalar.activation(out=f2[:], in_=f1[:], func=ACT.Copy, scale=k[:])
 
         start = 0
         for n, width in enumerate(OUT_CHUNKS):

@@ -36,7 +36,7 @@ def tile_attend_hvheldback_s_kernel(tc, query, query2, keys_words, keys_scales, 
         nc.sync.dma_start(offsets[:], offs)
 
         def load_rows(name, src):
-            raw = keep.tile([P, PACK, Q], F32, name=name + "_raw")
+            raw = keep.tile([P, PACK, Q], F32, name=name + "_raw", align_bytes=64)
             nc.sync.dma_start(out=raw[:], in_=src.rearrange("(p j) q -> p j q", j=PACK))
             return raw
 
@@ -55,7 +55,8 @@ def tile_attend_hvheldback_s_kernel(tc, query, query2, keys_words, keys_scales, 
 
         def interleave(name, raw, copy):
             grouped = keep.tile([P, Q, PACK], BF16, name=name + "_bf", align_bytes=64)
-            copy(out=grouped[:], in_=raw[:].rearrange("p j q -> p q j"))
+            copy(out=grouped[:].rearrange("p (c i) j -> p c j i", i=4),
+                 in_=raw[:].rearrange("p j (c i) -> p c j i", i=4))
             return grouped
 
         def quantise(name, grouped):
@@ -65,17 +66,22 @@ def tile_attend_hvheldback_s_kernel(tc, query, query2, keys_words, keys_scales, 
                                   in_=grouped[:].rearrange("p q j -> p (q j)"))
             return codes, scales
 
-        def gather(name, window, dtype, tag=""):
+        def gather(name, window, dtype, parts, tag=""):
             picked = sb(name, I, dtype, tag)
-            nc.vector.tensor_copy(picked[:], window.indirect(offsets[:]))
+            for part in parts:
+                listed = offsets[:, part.start // 16:part.stop // 16]
+                nc.vector.tensor_copy(picked[:, part], window.indirect(listed))
             return picked
 
-        def product(name, rows, words, scales):
+        def product(name, rows, words, scales, parts):
             bank = psum.tile([P, I], F32, name=name)
-            nc.tensor.matmul_mx(out=bank[:], lhsT=rows[0][:].bitcast(FP8X4), lhsT_scale=rows[1][:],
-                                rhs=words[:].bitcast(FP8X4), rhs_scale=scales[:], start=True, stop=True)
+            for part in parts:
+                nc.tensor.matmul_mx(out=bank[:, part], lhsT=rows[0][:].bitcast(FP8X4), lhsT_scale=rows[1][:],
+                                    rhs=words[:, part].bitcast(FP8X4), rhs_scale=scales[:, part],
+                                    start=True, stop=True)
             return bank
 
+        whole = slice(0, I)
         halves = (slice(0, I // 2), slice(I // 2, I))
 
         def col(name):
@@ -86,15 +92,15 @@ def tile_attend_hvheldback_s_kernel(tc, query, query2, keys_words, keys_scales, 
         nc.sync.dma_start(out=k[:], in_=strict)
         key_plane = load_scales("keys", keys_scales, nc.gpsimd, (nc.scalar, nc.scalar, nc.sync, nc.sync))
         key_words = load_words("keys", keys_words)
-        q_raw = load_rows("q", query)
-        dq2_raw = load_rows("dq2", dquery2)
-        go_raw = load_rows("go", gout)
         val_plane = load_scales("vals", vals_scales, nc.vector, (nc.sync,) * 4)
+        dq2_raw = load_rows("dq2", dquery2)
+        q_raw = load_rows("q", query)
+        go_raw = load_rows("go", gout)
         val_words = load_words("vals", vals_words)
         base_sb = sb("base_sb", T, F32)
         nc.sync.dma_start(out=base_sb[:], in_=base)
 
-        floor = col("floor")
+        floor = keep.tile([P, 1], F32, name="floor", align_bytes=64)
         nc.vector.memset(floor[:], LN_FLOOR)
         warm = col("warm")
         nc.scalar.activation(out=warm[:], in_=floor[:], func=ACT.Sigmoid)
@@ -102,41 +108,45 @@ def tile_attend_hvheldback_s_kernel(tc, query, query2, keys_words, keys_scales, 
         nc.vector.memset(placed[:], 0.0)
 
         q2 = quantise("q2", interleave("q2", q2_raw, nc.vector.tensor_copy))
-        q_bf = interleave("q", q_raw, nc.scalar.copy)
         dq2_bf = interleave("dq2", dq2_raw, nc.scalar.copy)
-        key_s = gather("key_s", key_plane[:], U8)
+        key_s = gather("key_s", key_plane[:], U8, [whole])
         nk1 = col("nk1")
         nc.vector.tensor_scalar(nk1[:], k[:], -1.0, -1.0, ALU.mult, ALU.add)
-        key_w = gather("key_w", key_words[:].bitcast(U32), U32)
-        b = product("b", q2, key_w, key_s)
-        sn = sb("sn", I, F32)
-        nc.scalar.activation(out=sn[:], in_=b[:], func=ACT.Sigmoid, scale=-1.0)
+        key_w = gather("key_w", key_words[:].bitcast(U32), U32, halves)
+        b = [product("b%d" % n, q2, key_w, key_s, [half]) for n, half in enumerate(halves)]
+        sn = sb("sn", I, F32, "dq2_raw")
+        for n, half in enumerate(halves):
+            nc.scalar.activation(out=sn[:, half], in_=b[n][:, half], func=ACT.Sigmoid, scale=-1.0)
         lsn = sb("lsn", I, F32)
-        nc.scalar.activation(out=lsn[:], in_=sn[:], func=ACT.Ln, bias=floor[:])
+        for half in halves:
+            nc.scalar.activation(out=lsn[:, half], in_=sn[:, half], func=ACT.Ln, bias=floor[:])
 
-        a = product("a", quantise("q", q_bf), key_w, key_s)
+        val_s = gather("val_s", val_plane[:], U8, [whole])
+        tb = product("tb", quantise("dq2", dq2_bf), key_w, key_s, [whole])
+        q_bf = interleave("q", q_raw, nc.vector.tensor_copy)
         go_bf = interleave("go", go_raw, nc.vector.tensor_copy)
-        tb = product("tb", quantise("dq2", dq2_bf), key_w, key_s)
-        val_s = gather("val_s", val_plane[:], U8)
+        a = product("a", quantise("q", q_bf), key_w, key_s, [whole])
         go = quantise("go", go_bf)
+        ts = sb("ts", I, F32)
+        nc.vector.scalar_tensor_tensor(ts[:], sn[:], -1.0, tb[:], ALU.add, ALU.mult)
 
         nsp = sb("nsp", I, F32)
-        nc.vector.scalar_tensor_tensor(nsp[:], b[:], -1.0, lsn[:], ALU.mult, ALU.min)
+        for n, half in enumerate(halves):
+            nc.vector.scalar_tensor_tensor(nsp[:, half], b[n][:, half], -1.0, lsn[:, half], ALU.mult, ALU.min)
         s = sb("s", I, F32)
-        nc.vector.scalar_tensor_tensor(s[:], nsp[:], k[:], a[:], ALU.mult, ALU.add)
+        for half in halves:
+            nc.vector.scalar_tensor_tensor(s[:, half], nsp[:, half], k[:], a[:, half], ALU.mult, ALU.add)
         nmax = col("nmax")
         nc.vector.tensor_reduce(nmax[:], s[:], AX.X, ALU.max, negate=True)
         p = sb("p", I, F32)
         z = col("z")
         nc.scalar.activation(out=p[:], in_=s[:], func=ACT.Exp, bias=nmax[:], accum_out=z[:])
 
-        ts = sb("ts", I, F32)
-        nc.vector.scalar_tensor_tensor(ts[:], sn[:], -1.0, tb[:], ALU.add, ALU.mult)
-        h = sb("h", I, F32)
+        h = sb("h", I, F32, "floor")
         nc.vector.scalar_tensor_tensor(h[:], ts[:], nk1[:], tb[:], ALU.mult, ALU.subtract)
 
-        val_w = gather("val_w", val_words[:].bitcast(U32), U32, "nsp")
-        c0 = product("c0", go, val_w, val_s)
+        val_w = gather("val_w", val_words[:].bitcast(U32), U32, halves, "nsp")
+        c0 = product("c0", go, val_w, val_s, halves)
 
         tp = sb("tp", I, F32)
         tz = col("tz")

@@ -19,7 +19,7 @@ AX = mybir.AxisListType
 P = 128
 PACK = 4
 LN_FLOOR = 2.0 ** -40
-OUT_CHUNKS = (640, 640, 512, 256)
+OUT_CHUNKS = (256, 384, 512, 512, 384)
 
 
 def tile_attend_hvheldback_s_kernel(tc, query, query2, keys_words, keys_scales, strict, gout,
@@ -147,6 +147,7 @@ def tile_attend_hvheldback_s_kernel(tc, query, query2, keys_words, keys_scales, 
 
         val_w = gather("val_w", val_words[:].bitcast(U32), U32, halves, "nsp")
         c0 = product("c0", go, val_w, val_s, halves)
+        c0_again = product("c0_again", go, val_w, val_s, [whole])
 
         tp = sb("tp", I, F32)
         tz = col("tz")
@@ -158,7 +159,7 @@ def tile_attend_hvheldback_s_kernel(tc, query, query2, keys_words, keys_scales, 
         nc.vector.scalar_tensor_tensor(pc[:], p[:], -1.0, c0[:], ALU.mult, ALU.mult, accum_out=ncz[:])
         cc = sb("cc", I, F32)
         for half in halves:
-            nc.scalar.activation(out=cc[:, half], in_=c0[:, half], func=ACT.Identity, scale=z[:], bias=ncz[:])
+            nc.scalar.activation(out=cc[:, half], in_=c0_again[:, half], func=ACT.Identity, scale=z[:], bias=ncz[:])
         tc0 = sb("tc0", I, F32)
         uz = col("uz")
         nc.vector.scalar_tensor_tensor(tc0[:], tp[:], 1.0, c0[:], ALU.mult, ALU.mult, accum_out=uz[:])

from contextlib import ExitStack

import concourse.mybir as mybir

D, T, I, Q = 512, 2048, 512, 128
FLOPS = 4 * 2 * D * Q * I

F32 = mybir.dt.float32
BF16 = mybir.dt.bfloat16
I32 = mybir.dt.int32
U32 = mybir.dt.uint32
U16 = mybir.dt.uint16
U8 = mybir.dt.uint8
FP8X4 = mybir.dt.float8_e4m3fn_x4
ALU = mybir.AluOpType
ACT = mybir.ActivationFunctionType
AX = mybir.AxisListType

P = 128
PACK = 4
LN_FLOOR = 2.0 ** -40
OUT_CHUNKS = (256, 384, 512, 512, 384)


def tile_attend_hvheldback_s_kernel(tc, query, query2, keys_words, keys_scales, strict, gout,
                                     vals_words, vals_scales, dquery2, base, offs, out):
    nc = tc.nc
    with ExitStack() as ctx:
        keep = ctx.enter_context(tc.tile_pool(name="keep", bufs=1))
        psum = ctx.enter_context(tc.psum_pool(name="psum", bufs=1))

        def sb(name, cols, dtype, tag=""):
            return keep.tile([P, cols], dtype, name=name, tag=tag or name, align_bytes=64)

        offsets = keep.tile([P, I // 16], U16, name="offsets")
        nc.sync.dma_start(offsets[:], offs)

        def load_rows(name, src):
            raw = keep.tile([P, PACK, Q], F32, name=name + "_raw", align_bytes=64)
            nc.sync.dma_start(out=raw[:], in_=src.rearrange("(p j) q -> p j q", j=PACK))
            return raw

        def load_words(name, src):
            words = sb(name + "_words", T, I32)
            nc.sync.dma_start(out=words[:], in_=src[0].rearrange("p n t -> p (n t)").bitcast(I32))
            return words

        def load_scales(name, src, clear, queues):
            plane = sb(name + "_scales", T, U8)
            clear.memset(plane[:].bitcast(I32), 0)
            for quad in range(4):
                queues[quad].dma_start(out=plane[32 * quad:32 * quad + 4, :].bitcast(I32),
                                in_=src[0, 4 * quad:4 * quad + 4, :].bitcast(I32))
            return plane

        def interleave(name, raw, copy):
            grouped = keep.tile([P, Q, PACK], BF16, name=name + "_bf", align_bytes=64)
            copy(out=grouped[:].rearrange("p (c i) j -> p c j i", i=4),
                 in_=raw[:].rearrange("p j (c i) -> p c j i", i=4))
            return grouped

        def quantise(name, grouped):
            codes = sb(name + "_codes", Q, U32)
            scales = sb(name + "_qs", Q, U8)
            nc.vector.quantize_mx(out=codes[:].bitcast(FP8X4), scales=scales[:],
                                  in_=grouped[:].rearrange("p q j -> p (q j)"))
            return codes, scales

        def gather(name, window, dtype, parts, tag=""):
            picked = sb(name, I, dtype, tag)
            for part in parts:
                listed = offsets[:, part.start // 16:part.stop // 16]
                nc.vector.tensor_copy(picked[:, part], window.indirect(listed))
            return picked

        def product(name, rows, words, scales, parts):
            bank = psum.tile([P, I], F32, name=name)
            for part in parts:
                nc.tensor.matmul_mx(out=bank[:, part], lhsT=rows[0][:].bitcast(FP8X4), lhsT_scale=rows[1][:],
                                    rhs=words[:, part].bitcast(FP8X4), rhs_scale=scales[:, part],
                                    start=True, stop=True)
            return bank

        whole = slice(0, I)
        halves = (slice(0, I // 2), slice(I // 2, I))

        def col(name):
            return keep.tile([P, 1], F32, name=name)

        q2_raw = load_rows("q2", query2)
        k = col("k")
        nc.sync.dma_start(out=k[:], in_=strict)
        key_plane = load_scales("keys", keys_scales, nc.gpsimd, (nc.scalar, nc.scalar, nc.sync, nc.sync))
        key_words = load_words("keys", keys_words)
        val_plane = load_scales("vals", vals_scales, nc.vector, (nc.sync,) * 4)
        dq2_raw = load_rows("dq2", dquery2)
        q_raw = load_rows("q", query)
        go_raw = load_rows("go", gout)
        val_words = load_words("vals", vals_words)
        base_sb = sb("base_sb", T, F32)
        nc.sync.dma_start(out=base_sb[:], in_=base)

        floor = keep.tile([P, 1], F32, name="floor", align_bytes=64)
        nc.vector.memset(floor[:], LN_FLOOR)
        warm = col("warm")
        nc.scalar.activation(out=warm[:], in_=floor[:], func=ACT.Sigmoid)
        placed = sb("placed", T, F32)
        nc.vector.memset(placed[:], 0.0)

        q2 = quantise("q2", interleave("q2", q2_raw, nc.vector.tensor_copy))
        dq2_bf = interleave("dq2", dq2_raw, nc.scalar.copy)
        key_s = gather("key_s", key_plane[:], U8, [whole])
        nk1 = col("nk1")
        nc.vector.tensor_scalar(nk1[:], k[:], -1.0, -1.0, ALU.mult, ALU.add)
        key_w = gather("key_w", key_words[:].bitcast(U32), U32, halves)
        b = [product("b%d" % n, q2, key_w, key_s, [half]) for n, half in enumerate(halves)]
        sn = sb("sn", I, F32, "dq2_raw")
        for n, half in enumerate(halves):
            nc.scalar.activation(out=sn[:, half], in_=b[n][:, half], func=ACT.Sigmoid, scale=-1.0)
        lsn = sb("lsn", I, F32)
        for half in halves:
            nc.scalar.activation(out=lsn[:, half], in_=sn[:, half], func=ACT.Ln, bias=floor[:])

        val_s = gather("val_s", val_plane[:], U8, [whole])
        tb = product("tb", quantise("dq2", dq2_bf), key_w, key_s, [whole])
        q_bf = interleave("q", q_raw, nc.vector.tensor_copy)
        go_bf = interleave("go", go_raw, nc.vector.tensor_copy)
        a = product("a", quantise("q", q_bf), key_w, key_s, [whole])
        go = quantise("go", go_bf)
        ts = sb("ts", I, F32)
        nc.vector.scalar_tensor_tensor(ts[:], sn[:], -1.0, tb[:], ALU.add, ALU.mult)

        nsp = sb("nsp", I, F32)
        for n, half in enumerate(halves):
            nc.vector.scalar_tensor_tensor(nsp[:, half], b[n][:, half], -1.0, lsn[:, half], ALU.mult, ALU.min)
        s = sb("s", I, F32)
        for half in halves:
            nc.vector.scalar_tensor_tensor(s[:, half], nsp[:, half], k[:], a[:, half], ALU.mult, ALU.add)
        nmax = col("nmax")
        nc.vector.tensor_reduce(nmax[:], s[:], AX.X, ALU.max, negate=True)
        p = sb("p", I, F32)
        z = col("z")
        nc.scalar.activation(out=p[:], in_=s[:], func=ACT.Exp, bias=nmax[:], accum_out=z[:])

        h = sb("h", I, F32, "floor")
        nc.vector.scalar_tensor_tensor(h[:], ts[:], nk1[:], tb[:], ALU.mult, ALU.subtract)

        val_w = gather("val_w", val_words[:].bitcast(U32), U32, halves, "nsp")
        c0 = product("c0", go, val_w, val_s, halves)
        c0_again = product("c0_again", go, val_w, val_s, [whole])

        tp = sb("tp", I, F32)
        tz = col("tz")
        nc.vector.scalar_tensor_tensor(tp[:], p[:], k[:], ts[:], ALU.mult, ALU.mult, accum_out=tz[:])
        rz = col("rz")
        nc.vector.reciprocal(rz[:], z[:])
        pc = sb("pc", I, F32)
        ncz = col("ncz")
        nc.vector.scalar_tensor_tensor(pc[:], p[:], -1.0, c0[:], ALU.mult, ALU.mult, accum_out=ncz[:])
        cc = sb("cc", I, F32)
        for half in halves:
            nc.scalar.activation(out=cc[:, half], in_=c0_again[:, half], func=ACT.Identity, scale=z[:], bias=ncz[:])
        tc0 = sb("tc0", I, F32)
        uz = col("uz")
        nc.vector.scalar_tensor_tensor(tc0[:], tp[:], 1.0, c0[:], ALU.mult, ALU.mult, accum_out=uz[:])
        tmean = col("tmean")
        nc.scalar.activation(out=tmean[:], in_=tz[:], func=ACT.Copy, scale=rz[:])
        v = col("v")
        nc.scalar.activation(out=v[:], in_=ncz[:], func=ACT.Identity, scale=tmean[:], bias=uz[:])
        sig = sb("sig", I, F32, "s")
        nc.scalar.activation(out=sig[:], in_=sn[:], func=ACT.Copy, scale=-512.0, bias=512.0)
        y = sb("y", I, F32)
        for half in halves:
            nc.vector.scalar_tensor_tensor(y[:, half], h[:, half], tmean[:], cc[:, half], ALU.add, ALU.mult)
        x = sb("x", I, F32)
        for half in halves:
            nc.vector.scalar_tensor_tensor(x[:, half], y[:, half], v[:], sig[:, half], ALU.add, ALU.mult)
        nc.vector.tensor_tensor(placed[:].indirect(offsets[:]), p[:], x[:], ALU.mult)

        f1 = col("f1")
        nc.scalar.activation(out=f1[:], in_=rz[:], func=ACT.Square)
        f2 = col("f2")
        nc.scalar.activation(out=f2[:], in_=f1[:], func=ACT.Copy, scale=k[:])

        start = 0
        for n, width in enumerate(OUT_CHUNKS):
            cols = slice(start, start + width)
            res = sb("res%d" % n, width, F32)
            nc.vector.scalar_tensor_tensor(res[:], placed[:, cols], f2[:], base_sb[:, cols], ALU.mult, ALU.add)
            nc.sync.dma_start(out=out[:, cols], in_=res[:])
            start = start + width
